import numpy as np
import ml_dtypes


def mxq(x, axis, fmt="e4m3"):
    dtype, down = {"e4m3": (ml_dtypes.float8_e4m3fn, 7), "e5m2": (ml_dtypes.float8_e5m2, 14)}[fmt]
    v = np.moveaxis(np.asarray(x, np.float32).astype(ml_dtypes.bfloat16).astype(np.float64), axis, -1)
    blocks = v.reshape(v.shape[:-1] + (-1, 32))
    amax = np.abs(blocks).max(-1, keepdims=True)
    byte = np.maximum(np.where(amax > 0, np.frexp(amax)[1] - 1 + 127, 0) - down, 1)
    scale = np.exp2(byte - 127.0)
    codes = (blocks / scale).astype(np.float32).astype(dtype).astype(np.float64)
    return np.moveaxis((codes * scale).reshape(v.shape), -1, axis)


WIDE = False


def mx_kscale(k):
    if not WIDE:
        return np.ones(k)
    levels = np.array([10, -10, 5, -5, 0])
    if k % 512:
        return np.exp2(np.random.permutation(np.resize(levels, k // 32))).repeat(32)
    a = np.empty((k // 512, 16))
    for p in range(k // 512):
        a[p, :8] = np.random.permutation(np.resize(levels, 8))
        for g in range(8):
            far = levels[np.abs(levels - a[p, g]) >= 10]
            a[p, g + 8] = far[np.random.randint(len(far))]
    return np.exp2(a.ravel()).repeat(32)


def f64(x):
    return np.asarray(x).astype(np.float64)


def striped(idx):
    return np.tile(idx.reshape(-1, 16).T, (8, 1)).astype(np.uint16)


def unstriped(offs):
    return offs[:16].T.reshape(-1).astype(np.int64)


def pack_weight(w):
    k, n = w.shape
    w = f64(np.asarray(w, np.float32).astype(ml_dtypes.bfloat16)).reshape(k // 32, 32, n)
    amax = np.abs(w).max(1)
    byte = np.clip(np.where(amax > 0, np.frexp(amax)[1] - 1 + 127 - 7, 1), 1, 254)
    scaled = (w * np.exp2(127.0 - byte)[:, None, :]).reshape(k, n).astype(np.float32)
    words = np.ascontiguousarray(scaled.reshape(k // 512, 128, 4, n).transpose(0, 1, 3, 2)).astype(ml_dtypes.float8_e4m3fn).view(np.uint8)
    return words, np.ascontiguousarray(byte.astype(np.uint8).reshape(k // 512, 16, n))


def unpack_weight(words, scales):
    g, p, n, _ = words.shape
    vals = np.ascontiguousarray(words).view(ml_dtypes.float8_e4m3fn).astype(np.float64) * np.repeat(np.exp2(scales.astype(np.float64) - 127.0), 8, axis=1)[..., None]
    return vals.transpose(0, 1, 3, 2).reshape(g * 512, n)


E2M1 = np.array([0.0, 0.5, 1.0, 1.5, 2.0, 3.0, 4.0, 6.0, -0.0, -0.5, -1.0, -1.5, -2.0, -3.0, -4.0, -6.0])


def pack_fp4(w):
    k, n = w.shape
    w = f64(np.asarray(w, np.float32).astype(ml_dtypes.bfloat16)).reshape(k // 32, 32, n)
    amax = np.abs(w).max(1)
    mant, ex = np.frexp(amax / 6.0)
    byte = np.clip(np.where(amax > 0, np.where(mant > 0.5, ex, ex - 1) + 127, 1), 1, 254)
    scaled = (w * np.exp2(127.0 - byte)[:, None, :]).reshape(k, n).astype(np.float32)
    c = np.ascontiguousarray(scaled.reshape(k // 512, 128, 4, n).transpose(0, 1, 3, 2)).astype(ml_dtypes.float4_e2m1fn).view(np.uint8) & 0xF
    words = (c[..., 0::2] | (c[..., 1::2] << 4)).reshape(k // 512, 128, 2 * n)
    return np.ascontiguousarray(words), np.ascontiguousarray(byte.astype(np.uint8).reshape(k // 512, 16, n))


def unpack_fp4(words, scales):
    g, _, n = scales.shape
    words = np.ascontiguousarray(words).reshape(g, 128, n, 2)
    nib = np.empty((g, 128, n, 4), np.uint8)
    nib[..., 0::2] = words & 0xF
    nib[..., 1::2] = words >> 4
    vals = E2M1[nib] * np.repeat(np.exp2(scales.astype(np.float64) - 127.0), 8, axis=1)[..., None]
    return vals.transpose(0, 1, 3, 2).reshape(g * 512, n)


def planes(y):
    n, m = y.shape
    v = y.astype(np.float32).astype(ml_dtypes.bfloat16).astype(np.float64).reshape(n // 32, 32, m)
    top = np.abs(v).max(1)
    byte = np.clip(np.where(top > 0, np.frexp(top)[1] - 1 + 127 - 7, 1), 1, 254)
    codes = (v * np.exp2(127.0 - byte)[:, None, :]).reshape(n, m).astype(np.float32).astype(ml_dtypes.float8_e4m3fn).view(np.uint8)
    words = codes.reshape(n // 512, 128, 4, m).transpose(0, 1, 3, 2)
    return np.ascontiguousarray(words), np.ascontiguousarray(byte.astype(np.uint8).reshape(n // 512, 16, m))


K, T, S, H, Z, W = 512, 1024, 512, 512, 512, 2048
P = 2 ** 7


def setup_inputs():
    n = np.random.standard_normal
    s = mx_kscale(K)[:, None]
    u = mx_kscale(H)
    packed_xT = pack_weight(n((K, T)) * s)
    packed_w1 = pack_fp4(n((K, H)) / np.sqrt(K) / s)
    packed_eT = pack_weight(n((K, W)) * s)
    packed_w2 = pack_fp4(n((K, H)) / np.sqrt(K) / s)
    return {
        "x_words": packed_xT[0],
        "x_scales": packed_xT[1],
        "w1_words": packed_w1[0],
        "w1_scales": packed_w1[1],
        "e_words": packed_eT[0],
        "e_scales": packed_eT[1],
        "w2_words": packed_w2[0],
        "w2_scales": packed_w2[1],
        "unit": (np.random.uniform(0.6, 1.4, (H, 1)) * u[:, None]).astype(np.float32),
        "unit2": (np.random.uniform(0.6, 1.4, (H, 1)) / np.sqrt(H) / u[:, None]).astype(np.float32),
        "fare": (np.tile(np.random.uniform(0.1, 0.8, W), (P, 1))).astype(np.float32),
        "offs": striped(np.random.permutation(T)[:S]),
        "dst": striped(np.random.permutation(W)[:Z]),
        "hb": striped(np.random.permutation(S)),
        "tr1": striped(np.random.permutation(Z)),
        "tr2": striped(np.random.permutation(Z)),
    }


def reference(x_words, x_scales, w1_words, w1_scales, e_words, e_scales, w2_words, w2_scales, unit, unit2, fare, offs, dst, hb, tr1, tr2):
    xq = unpack_weight(x_words, x_scales)[:, unstriped(offs)]
    y = unpack_fp4(w1_words, w1_scales).T @ xq
    yh = y[:, unstriped(hb)]
    acc_ = np.maximum(y, 0.8 * yh)
    hid = f64(unit) * acc_
    e_dst = unpack_weight(e_words, e_scales)[:, unstriped(dst)]
    ye = unpack_fp4(w2_words, w2_scales).T @ e_dst
    hid2 = f64(unit2) * ye
    sc = mxq(hid, 0, "e4m3").T @ mxq(hid2, 0, "e4m3")
    sa = sc[:, unstriped(tr1)]
    sb = 0.5 * sc[:, unstriped(tr2)]
    cst = np.minimum(sc, sa + sb + f64(fare)[:1][:, unstriped(dst)])
    va = cst[:, unstriped(tr1)]
    out_0 = cst - (0.5 * va)
    return (out_0,) + planes(out_0)

from contextlib import ExitStack

import concourse.mybir as mybir
from concourse.masks import make_identity

F32 = mybir.dt.float32
BF16 = mybir.dt.bfloat16
I32 = mybir.dt.int32
U32 = mybir.dt.uint32
U16 = mybir.dt.uint16
U8 = mybir.dt.uint8
FP8X4 = mybir.dt.float8_e4m3fn_x4
FP4X4 = mybir.dt.float4_e2m1fn_x4
ALU = mybir.AluOpType
ACT = mybir.ActivationFunctionType

P = 128
PACK = 4
N = 512
HALF = N // 2
T_ORIGINS = 1024
T_DESTS = 2048
FLOPS = 3 * 2 * 512 * 512 * 512


def tile_picked_yodtrn_sav_po_kernel(
    tc, x_words, x_scales, w1_words, w1_scales, e_words, e_scales, w2_words, w2_scales,
    unit, unit2, fare, offs, dst, hb, tr1, tr2, out_0, out_1, out_2,
):
    nc = tc.nc
    with ExitStack() as ctx:
        keep = ctx.enter_context(tc.tile_pool(name="keep", bufs=1))
        psum = ctx.enter_context(tc.psum_pool(name="psum", bufs=1))

        def sb(shape, dtype, name, tag=None):
            return keep.tile(shape, dtype, name=name, tag=tag or name, align_bytes=64)

        def cols(h):
            return slice(h * HALF, (h + 1) * HALF)

        def entries(lst, h):
            return lst[:, h * (HALF // 16) : (h + 1) * (HALF // 16)]

        def load_scale_rows(queue, plane, src, q):
            queue.dma_start(
                out=plane[:].bitcast(I32)[32 * q : 32 * q + 4, :],
                in_=src[0].bitcast(I32)[4 * q : 4 * q + 4, :],
            )

        def load_list(src, name):
            lst = keep.tile([P, N // 16], U16, name=name)
            nc.sync.dma_start(lst[:], src)
            return lst

        def load_unit(queue, src, rows):
            queue.dma_start(
                out=rows[0:PACK, :].rearrange("t (g r) -> t g r", r=8),
                in_=src.rearrange("(g t r) o -> t g (r o)", t=PACK, r=8),
            )

        def turn_unit(rows, bank_name):
            turned = psum.tile([P, P], F32, name=bank_name)
            nc.tensor.transpose(turned[:], rows[:], ident[:])
            return turned[:, 0:PACK]

        xs = sb([P, T_ORIGINS], U8, "xs")
        w1s = sb([P, N], U8, "w1s")
        es = sb([P, T_DESTS], U8, "es")
        w2s = sb([P, N], U8, "w2s")
        u1_rows = sb([P, P], F32, "u1_rows")
        u2_rows = sb([P, P], F32, "u2_rows")
        nc.vector.memset(xs[:].bitcast(I32), 0)
        nc.gpsimd.memset(w1s[:].bitcast(I32), 0)
        nc.gpsimd.memset(u1_rows[:], 0.0)
        nc.vector.memset(es[:].bitcast(I32), 0)
        nc.gpsimd.memset(w2s[:].bitcast(I32), 0)
        nc.gpsimd.memset(u2_rows[:], 0.0)
        ident = sb([P, P], F32, "ident")
        make_identity(nc, ident[:])

        xw = sb([P, T_ORIGINS], I32, "xw", tag="table")
        ew = sb([P, T_DESTS], I32, "ew")
        w1w = sb([P, 2 * N], U8, "w1w")
        w2w = sb([P, 2 * N], U8, "w2w")

        offs_sb = load_list(offs, "offs_sb")
        nc.sync.dma_start(out=xw[:], in_=x_words[0].rearrange("p n t -> p (n t)").bitcast(I32))
        nc.scalar.dma_start(out=w1w[:].bitcast(I32), in_=w1_words[0].bitcast(I32))
        for q in range(4):
            load_scale_rows(nc.scalar if q < 2 else nc.sync, xs, x_scales, q)
        nc.sync.dma_start(out=ew[:], in_=e_words[0].rearrange("p n t -> p (n t)").bitcast(I32))
        load_scale_rows(nc.sync, w1s, w1_scales, 0)
        load_unit(nc.scalar, unit, u1_rows)
        for q in range(1, 4):
            load_scale_rows(nc.sync, w1s, w1_scales, q)
        dst_sb = load_list(dst, "dst_sb")
        load_scale_rows(nc.sync, es, e_scales, 0)
        nc.sync.dma_start(out=w2w[:].bitcast(I32), in_=w2_words[0].bitcast(I32))
        for q in range(1, 4):
            load_scale_rows(nc.sync, es, e_scales, q)
        for q in range(4):
            load_scale_rows(nc.sync, w2s, w2_scales, q)
        hb_sb = load_list(hb, "hb_sb")
        load_unit(nc.sync, unit2, u2_rows)
        tr1_sb = load_list(tr1, "tr1_sb")
        tr2_sb = load_list(tr2, "tr2_sb")

        def gather_packed(words, plane, lst, name):
            gw = sb([P, N], U32, name + "_gw")
            gs = sb([P, N], U8, name + "_gs")
            for h in range(2):
                nc.vector.tensor_copy(gw[:, cols(h)], words[:].bitcast(U32).indirect(entries(lst, h)))
                nc.vector.tensor_copy(gs[:, cols(h)], plane[:].indirect(entries(lst, h)))
            return gw, gs

        def deal(src, width, name):
            dealt = sb([P, width], U8, name)
            nc.gpsimd.tensor_copy(
                out=dealt[:].bitcast(I32).rearrange("p (t g r) -> p t g r", t=PACK, g=16),
                in_=src[:].bitcast(I32).rearrange("p (g t r) -> p t g r", t=PACK, g=16),
            )
            return dealt

        xgw, xgs = gather_packed(xw, xs, offs_sb, "x")
        fare_sb = sb([P, T_DESTS], F32, "fare_sb", tag="table")
        nc.sync.dma_start(out=fare_sb[:], in_=fare)
        w1wd = deal(w1w, 2 * N, "w1wd")
        w1sd = deal(w1s, N, "w1sd")
        u1_abs = sb([P, PACK], F32, "u1_abs")
        u1 = turn_unit(u1_rows, "ebank2")
        nc.scalar.activation(u1_abs[:], u1, ACT.Abs)
        u1_sign2 = sb([P, PACK], F32, "u1_sign2")
        nc.vector.tensor_scalar(u1_sign2[:], u1, 0.0, 2.0, ALU.is_ge, ALU.mult)

        y_banks = [psum.tile([P, N], F32, name="bank%d" % t) for t in range(PACK)]
        for h in range(2):
            for t in range(PACK):
                nc.tensor.matmul_mx(
                    out=y_banks[t][:, cols(h)],
                    lhsT=w1wd[:, 2 * P * t : 2 * P * (t + 1)].bitcast(FP4X4),
                    lhsT_scale=w1sd[:, P * t : P * (t + 1)],
                    rhs=xgw[:, cols(h)].bitcast(FP8X4),
                    rhs_scale=xgs[:, cols(h)],
                    start=True, stop=True,
                )
        y = sb([P, PACK, N], F32, "y")
        for t in range(PACK):
            nc.scalar.activation(y[:, t, :], y_banks[t][:], ACT.Copy, scale=u1_abs[:, t : t + 1])
        yh = [sb([P, PACK, HALF], F32, "yh%d" % h) for h in range(2)]
        for h in range(2):
            for t in range(PACK):
                nc.scalar.activation(yh[h][:, t, :], y[:, t, :].indirect(entries(hb_sb, h)), ACT.Copy, scale=0.8)

        egw, egs = gather_packed(ew, es, dst_sb, "e")
        w2wd = deal(w2w, 2 * N, "w2wd")
        w2sd = deal(w2s, N, "w2sd")
        u2 = turn_unit(u2_rows, "ebank3")
        u2_signed = sb([P, PACK], F32, "u2_signed")
        nc.vector.scalar_tensor_tensor(u2_signed[:], u1_sign2[:], -1.0, u2, ALU.add, ALU.mult)

        hid2 = sb([P, N, PACK], BF16, "hid2")
        for b in range(4):
            bank = psum.tile([P, PACK, P], F32, name="ebank%d" % b)
            for t in range(PACK):
                nc.tensor.matmul_mx(
                    out=bank[:, t, :],
                    lhsT=w2wd[:, 2 * P * t : 2 * P * (t + 1)].bitcast(FP4X4),
                    lhsT_scale=w2sd[:, P * t : P * (t + 1)],
                    rhs=egw[:, P * b : P * (b + 1)].bitcast(FP8X4),
                    rhs_scale=egs[:, P * b : P * (b + 1)],
                    start=True, stop=True,
                )
            nc.vector.tensor_tensor(
                hid2[:, P * b : P * (b + 1), :],
                bank[:].rearrange("p t n -> p n t"),
                u2_signed[:].unsqueeze(1).broadcast_to([P, P, PACK]),
                ALU.mult,
            )
        h2w = sb([P, N], U32, "h2w")
        h2s = sb([P, N], U8, "h2s")
        nc.vector.quantize_mx(out=h2w[:].bitcast(FP8X4), scales=h2s[:], in_=hid2[:].rearrange("p n t -> p (n t)"))

        hid = sb([P, PACK, P, PACK], BF16, "hid")
        for h in range(2):
            nc.vector.tensor_tensor(
                hid[:, :, h * (P // 2) : (h + 1) * (P // 2), :].rearrange("p s m t -> p m t s"),
                yh[h][:].rearrange("p t (m s) -> p m t s", s=PACK),
                y[:, :, cols(h)].rearrange("p t (m s) -> p m t s", s=PACK),
                ALU.max,
            )
        fare_g = sb([P, N], F32, "fare_g")
        nc.scalar.activation(fare_g[:], fare_sb[:].indirect(dst_sb[:]), ACT.Copy)

        hw = sb([P, N], U32, "hw")
        hs = sb([P, N], U8, "hs")
        sc_banks = []
        for s in range(PACK):
            nc.vector.quantize_mx(
                out=hw[:, P * s : P * (s + 1)].bitcast(FP8X4),
                scales=hs[:, P * s : P * (s + 1)],
                in_=hid[:, s, :, :].rearrange("p m t -> p (m t)"),
            )
            bank = psum.tile([P, N], F32, name="bank%d" % s)
            nc.tensor.matmul_mx(
                out=bank[:],
                lhsT=hw[:, P * s : P * (s + 1)].bitcast(FP8X4),
                lhsT_scale=hs[:, P * s : P * (s + 1)],
                rhs=h2w[:].bitcast(FP8X4),
                rhs_scale=h2s[:],
                start=True, stop=True,
            )
            sc_banks.append(bank)

        sc = [sb([P, N], F32, "sc%d" % s) for s in range(PACK)]
        via1 = [sb([P, N], F32, "via1_%d" % s) for s in range(PACK)]
        via2 = [sb([P, N], F32, "via2_%d" % s) for s in range(PACK)]
        via = [sb([P, N], F32, "via_%d" % s) for s in range(PACK)]
        cst = [sb([P, N], F32, "cst%d" % s) for s in range(PACK)]
        va = [sb([P, N], F32, "va%d" % s) for s in range(PACK)]
        res = sb([P, PACK, N], F32, "res")
        out_rows = out_0.rearrange("(p s) c -> p s c", s=PACK)

        def costs(s):
            nc.scalar.copy(sc[s][:], sc_banks[s][:])
            for h in range(2):
                nc.scalar.activation(via2[s][:, cols(h)], sc[s][:].indirect(entries(tr2_sb, h)), ACT.Copy)
            for h in range(2):
                nc.vector.tensor_tensor(
                    via1[s][:, cols(h)], sc[s][:].indirect(entries(tr1_sb, h)), fare_g[:, cols(h)], ALU.add
                )
            for h in range(2):
                nc.vector.scalar_tensor_tensor(
                    via[s][:, cols(h)], via2[s][:, cols(h)], 0.5, via1[s][:, cols(h)], ALU.mult, ALU.add
                )
            for h in range(2):
                nc.vector.tensor_tensor(cst[s][:, cols(h)], via[s][:, cols(h)], sc[s][:, cols(h)], ALU.min)

        def result(s):
            for h in range(2):
                picked = cst[s][:].indirect(entries(tr1_sb, h))
                if s == PACK - 1 and h == 1:
                    nc.vector.tensor_copy(va[s][:, cols(h)], picked)
                else:
                    nc.scalar.activation(va[s][:, cols(h)], picked, ACT.Copy)
            for h in range(2):
                nc.vector.scalar_tensor_tensor(
                    res[:, s, cols(h)], va[s][:, cols(h)], -0.5, cst[s][:, cols(h)], ALU.mult, ALU.add
                )
            nc.sync.dma_start(out=out_rows[:, s, :], in_=res[:, s, :])

        costs(0)
        for s in range(1, PACK):
            costs(s)
            result(s - 1)
        result(PACK - 1)

        ow = sb([P, N], I32, "ow")
        osc = sb([P, N], U8, "osc")
        out_words = out_1[0].rearrange("p n t -> p (n t)").bitcast(I32)
        rb = [sb([P, HALF, PACK], BF16, "rb%d" % h) for h in range(2)]
        for h in range(2):
            (nc.vector.tensor_copy if h else nc.scalar.copy)(
                out=rb[h][:].rearrange("p (c i) s -> p c s i", i=4),
                in_=res[:, :, cols(h)].rearrange("p s (c i) -> p c s i", i=4),
            )
        for h in (1, 0):
            nc.vector.quantize_mx(
                out=ow[:, cols(h)].bitcast(FP8X4),
                scales=osc[:, cols(h)],
                in_=rb[h][:].rearrange("p n s -> p (n s)"),
            )
            nc.sync.dma_start(out=out_words[:, cols(h)], in_=ow[:, cols(h)])
        for q in range(4):
            (nc.sync if q % 2 else nc.scalar).dma_start(
                out=out_2[0].bitcast(I32)[4 * q : 4 * q + 4, :],
                in_=osc[:].bitcast(I32)[32 * q : 32 * q + 4, :],
            )
